import numpy as np
import ml_dtypes


def mxq(x, axis, fmt="e4m3"):
    dtype, down = {"e4m3": (ml_dtypes.float8_e4m3fn, 7), "e5m2": (ml_dtypes.float8_e5m2, 14)}[fmt]
    v = np.moveaxis(np.asarray(x, np.float32).astype(ml_dtypes.bfloat16).astype(np.float64), axis, -1)
    blocks = v.reshape(v.shape[:-1] + (-1, 32))
    amax = np.abs(blocks).max(-1, keepdims=True)
    byte = np.maximum(np.where(amax > 0, np.frexp(amax)[1] - 1 + 127, 0) - down, 1)
    scale = np.exp2(byte - 127.0)
    codes = (blocks / scale).astype(np.float32).astype(dtype).astype(np.float64)
    return np.moveaxis((codes * scale).reshape(v.shape), -1, axis)


WIDE = False


def mx_kscale(k):
    if not WIDE:
        return np.ones(k)
    levels = np.array([24, -24, 12, -12, 0])
    if k % 512:
        return np.exp2(np.random.permutation(np.resize(levels, k // 32))).repeat(32)
    a = np.empty((k // 512, 16))
    for p in range(k // 512):
        a[p, :8] = np.random.permutation(np.resize(levels, 8))
        for g in range(8):
            far = levels[np.abs(levels - a[p, g]) >= 10]
            a[p, g + 8] = far[np.random.randint(len(far))]
    return np.exp2(a.ravel()).repeat(32)


def f64(x):
    return np.asarray(x).astype(np.float64)


def striped8(idx):
    return np.concatenate([v.reshape(-1, 16).T for v in idx]).astype(np.uint16)


def unstriped8(offs):
    return np.stack([offs[16 * g:16 * g + 16].T.reshape(-1) for g in range(8)]).astype(np.int64)


E2M1 = np.array([0.0, 0.5, 1.0, 1.5, 2.0, 3.0, 4.0, 6.0, -0.0, -0.5, -1.0, -1.5, -2.0, -3.0, -4.0, -6.0])


def pack_weight(w, fmt):
    k, n = w.shape
    w = f64(np.asarray(w, np.float32).astype(ml_dtypes.bfloat16)).reshape(k // 32, 32, n)
    amax = np.abs(w).max(1)
    if fmt == "e4m3":
        byte = np.frexp(amax)[1] - 1 + 127 - 7
    else:
        mant, ex = np.frexp(amax / 6.0)
        byte = np.where(mant > 0.5, ex, ex - 1) + 127
    byte = np.clip(np.where(amax > 0, byte, 1), 1, 254)
    scaled = (w * np.exp2(127.0 - byte)[:, None, :]).reshape(k, n).astype(np.float32)
    by_word = np.ascontiguousarray(scaled.reshape(k // 512, 128, 4, n).transpose(0, 1, 3, 2))
    if fmt == "e4m3":
        words = by_word.astype(ml_dtypes.float8_e4m3fn).view(np.uint8)
    else:
        c = by_word.astype(ml_dtypes.float4_e2m1fn).view(np.uint8) & 0xF
        words = (c[..., 0::2] | (c[..., 1::2] << 4)).reshape(k // 512, 128, 2 * n)
    return np.ascontiguousarray(words), np.ascontiguousarray(byte.astype(np.uint8).reshape(k // 512, 16, n))


def unpack_weight(words, scales, fmt):
    g, _, n = scales.shape
    words = np.ascontiguousarray(words).reshape(g, 128, n, -1)
    if fmt == "e4m3":
        vals = words.view(ml_dtypes.float8_e4m3fn).astype(np.float64)
    else:
        nib = np.empty((g, 128, n, 4), np.uint8)
        nib[..., 0::2] = words & 0xF
        nib[..., 1::2] = words >> 4
        vals = E2M1[nib]
    vals = vals * np.repeat(np.exp2(scales.astype(np.float64) - 127.0), 8, axis=1)[..., None]
    return vals.transpose(0, 1, 3, 2).reshape(g * 512, n)


def planes(y):
    n, m = y.shape
    v = y.astype(np.float32).astype(ml_dtypes.bfloat16).astype(np.float64).reshape(n // 32, 32, m)
    top = np.abs(v).max(1)
    byte = np.clip(np.where(top > 0, np.frexp(top)[1] - 1 + 127 - 7, 1), 1, 254)
    codes = (v * np.exp2(127.0 - byte)[:, None, :]).reshape(n, m).astype(np.float32).astype(ml_dtypes.float8_e4m3fn).view(np.uint8)
    words = codes.reshape(n // 512, 128, 4, m).transpose(0, 1, 3, 2)
    return np.ascontiguousarray(words), np.ascontiguousarray(byte.astype(np.uint8).reshape(n // 512, 16, m))


def sigm(f):
    return 1.0 / (1.0 + np.exp(-np.maximum(f, -700.0)))


K, N, T, J = 1024, 512, 2048, 1024


def setup_inputs():
    n = np.random.standard_normal
    s = mx_kscale(K)[:, None]
    p_wk = pack_weight(n((K, N)) / np.sqrt(K) / s, "e4m3")
    p_wv4 = pack_weight(n((K, N)) / np.sqrt(K) / s, "e2m1")
    return {
        "xT": (n((K, T)) * s).astype(np.float32),
        "wgt": np.repeat(np.random.uniform(0.5, 2.0, (8, J)), 16, axis=0).astype(np.float32),
        "wk_words": p_wk[0],
        "wk_scales": p_wk[1],
        "wv4_words": p_wv4[0],
        "wv4_scales": p_wv4[1],
        "wvd": (0.4 * (n((K, N)) / np.sqrt(K) / s)).astype(np.float32),
        "bg": (0.3 * n(N) - 1.0).astype(np.float32),
        "res": (n((N, J))).astype(np.float32),
        "offs": striped8(np.stack([np.random.permutation(T)[:J] for _ in range(8)])),
    }


def reference(xT, wgt, wk_words, wk_scales, wv4_words, wv4_scales, wvd, bg, res, offs):
    idx = unstriped8(offs)
    rows = np.arange(K)
    xg = f64(wgt)[rows // 4 % 128] * f64(xT)[rows[:, None], idx[rows % 512 // 64]]
    xT_ = mxq(xg, 0, "e4m3")
    wk_ = unpack_weight(wk_words, wk_scales, "e4m3")
    wv4_ = unpack_weight(wv4_words, wv4_scales, "e2m1")
    wvd_ = mxq(f64(wvd), 0, "e4m3")
    ke = wk_.T @ xT_
    ve = wv4_.T @ xT_ + wvd_.T @ xT_
    gate = sigm(ke + f64(bg)[:, None])
    out_0 = f64(res) + gate * (ve - f64(res))
    return (out_0,) + planes(out_0)

@@ -1,0 +1,243 @@
+from contextlib import ExitStack
+
+import concourse.mybir as mybir
+
+K, N, T, J = 1024, 512, 2048, 1024
+FLOPS = 3 * 2 * K * N * J
+
+F32 = mybir.dt.float32
+BF16 = mybir.dt.bfloat16
+I32 = mybir.dt.int32
+U32 = mybir.dt.uint32
+U16 = mybir.dt.uint16
+U8 = mybir.dt.uint8
+FP8X4 = mybir.dt.float8_e4m3fn_x4
+FP4X4 = mybir.dt.float4_e2m1fn_x4
+ALU = mybir.AluOpType
+ACT = mybir.ActivationFunctionType
+
+P = 128
+PACK = 4
+K_PASS = P * PACK
+PASSES = K // K_PASS
+W = 256
+PARTS = J // W
+WK_ROW = 4
+
+
+def tile_list_dl_hwayP_kernel(
+    tc, xT, wgt, wk_words, wk_scales, wv4_words, wv4_scales, wvd, bg, res, offs, out_0, out_1, out_2
+):
+    nc = tc.nc
+    with ExitStack() as ctx:
+        held = ctx.enter_context(tc.tile_pool(name="held", bufs=1))
+        ring = ctx.enter_context(tc.tile_pool(name="ring", bufs=2))
+        psum = ctx.enter_context(tc.psum_pool(name="psum", bufs=2))
+
+        offsets = held.tile([P, J // 16], U16, name="offsets")
+        nc.sync.dma_start(offsets[:], offs)
+
+        raw_scales = held.tile([P, PASSES * N], U8, name="raw_scales", align_bytes=64)
+        nc.gpsimd.memset(raw_scales[:].bitcast(I32), 0)
+
+        head_w = held.tile([P, J], F32, name="head_w")
+        planes = [held.tile([P, T], F32, name="plane%d" % q) for q in range(PASSES * PACK)]
+        x_rows = xT.rearrange("(a p i) t -> a i p t", a=PASSES, i=PACK)
+
+        def load_plane(a, i):
+            nc.sync.dma_start(planes[PACK * a + i][:], x_rows[a, i])
+
+        wk_raw = held.tile([P, PASSES, N], I32, name="wk_raw")
+        wv4_raw = held.tile([P, PASSES, N // 2], I32, name="wv4_raw")
+        wvd_raw = [held.tile([P, PACK, N], F32, name="wvd_raw%d" % a) for a in range(PASSES)]
+        bias = held.tile([P, PACK], F32, name="bias")
+        carried = [held.tile([P, PACK, W], F32, name="carried%d" % h) for h in range(PARTS)]
+        res_rows = res.rearrange("(p t) j -> p t j", t=PACK)
+        out_rows = out_0.rearrange("(p t) j -> p t j", t=PACK)
+
+        def load_scales(src, row0, q):
+            dst = raw_scales[32 * q + row0 : 32 * q + row0 + 4, :].bitcast(I32)
+            nc.sync.dma_start(
+                dst.rearrange("r (a n) -> r a n", a=PASSES),
+                src[:, 4 * q : 4 * q + 4, :].bitcast(I32).rearrange("a r n -> r a n"),
+            )
+
+        def load_wvd(a):
+            nc.sync.dma_start(
+                wvd_raw[a][:], wvd[a * K_PASS : (a + 1) * K_PASS, :].rearrange("(p i) n -> p i n", i=PACK)
+            )
+
+        nc.sync.dma_start(head_w[:, 0 : J // 2], wgt[:, 0 : J // 2])
+        load_plane(0, 0)
+        nc.sync.dma_start(head_w[:, J // 2 : J], wgt[:, J // 2 : J])
+        for i in range(PACK):
+            if i:
+                load_plane(0, i)
+            load_scales(wk_scales, WK_ROW, i)
+            load_scales(wv4_scales, 0, i)
+        nc.sync.dma_start(bias[:], bg.rearrange("(p t) -> p t", t=PACK))
+        nc.sync.dma_start(wk_raw[:], wk_words.rearrange("a p n i -> p a (n i)").bitcast(I32))
+        nc.sync.dma_start(wv4_raw[:], wv4_words.rearrange("a p b -> p a b").bitcast(I32))
+        load_wvd(0)
+        load_plane(1, 0)
+        load_wvd(1)
+        for i in range(1, PACK):
+            load_plane(1, i)
+        for h in range(PARTS):
+            nc.sync.dma_start(carried[h][:], res_rows[:, :, h * W : (h + 1) * W])
+
+        def interleave(dst, src):
+            nc.scalar.copy(
+                out=dst.rearrange("p (c u i) -> p c i u", u=4, i=PACK),
+                in_=src.rearrange("p i (c u) -> p c i u", u=4),
+            )
+
+        picked = [held.tile([P, PACK, J], F32, name="picked%d" % a) for a in range(PASSES)]
+        x_codes = {}
+        x_scales = {}
+
+        def gather(a, i, pieces):
+            width = J // pieces
+            for c0 in range(0, J, width):
+                nc.vector.tensor_tensor(
+                    out=picked[a][:, i, c0 : c0 + width],
+                    in0=planes[PACK * a + i][:].indirect(offsets[:, c0 // 16 : (c0 + width) // 16]),
+                    in1=head_w[:, c0 : c0 + width],
+                    op=ALU.mult,
+                )
+
+        def quantize_x(a, c0, width):
+            rounded = ring.tile([P, PACK * width], BF16, name="rounded", align_bytes=64)
+            interleave(rounded[:], picked[a][:, :, c0 : c0 + width])
+            codes = held.tile([P, width], U32, name="x_codes%d_%d" % (a, c0), align_bytes=64)
+            scales = held.tile([P, width], U8, name="x_scales%d_%d" % (a, c0), align_bytes=64)
+            nc.vector.quantize_mx(out=codes[:].bitcast(FP8X4), scales=scales[:], in_=rounded[:])
+            for s0 in range(0, width, W):
+                x_codes[a, (c0 + s0) // W] = codes[:, s0 : s0 + W]
+                x_scales[a, (c0 + s0) // W] = scales[:, s0 : s0 + W]
+
+        wk_codes = held.tile([P, PASSES, N], U32, name="wk_codes", align_bytes=64)
+        wv4_codes = held.tile([P, PASSES, 2 * N], U8, name="wv4_codes", align_bytes=64)
+        w_scales = held.tile([P, PASSES * N], U8, name="w_scales", align_bytes=64)
+        wvd_codes = [held.tile([P, N], U32, name="wvd_codes%d" % a, align_bytes=64) for a in range(PASSES)]
+        wvd_scales = [held.tile([P, N], U8, name="wvd_scales%d" % a, align_bytes=64) for a in range(PASSES)]
+
+        def deal_packed():
+            for a in range(PASSES):
+                nc.scalar.copy(
+                    out=wk_codes[:, a, :].rearrange("p (t c u) -> p c t u", t=PACK, u=4),
+                    in_=wk_raw[:, a, :].bitcast(U32).rearrange("p (c u t) -> p c t u", t=PACK, u=4),
+                )
+                nc.scalar.copy(
+                    out=wv4_codes[:, a, :].bitcast(U16).rearrange("p (t c u) -> p c t u", t=PACK, u=8),
+                    in_=wv4_raw[:, a, :].bitcast(U16).rearrange("p (c u t) -> p c t u", t=PACK, u=8),
+                )
+            nc.vector.tensor_copy(
+                out=w_scales[:].rearrange("p (a t c u) -> p a c t u", a=PASSES, t=PACK, u=16),
+                in_=raw_scales[:].rearrange("p (a c u t) -> p a c t u", a=PASSES, t=PACK, u=16),
+            )
+
+        def quantize_wvd(a):
+            rounded = ring.tile([P, PACK * N], BF16, name="rounded", align_bytes=64)
+            nc.scalar.copy(
+                out=rounded[:].rearrange("p (t m i) -> p m i t", t=PACK, i=PACK),
+                in_=wvd_raw[a][:].rearrange("p i (m t) -> p m i t", t=PACK),
+            )
+            nc.vector.quantize_mx(out=wvd_codes[a][:].bitcast(FP8X4), scales=wvd_scales[a][:], in_=rounded[:])
+
+        out_codes = held.tile([P, J], U32, name="out_codes", align_bytes=64)
+        out_scales = held.tile([P, J], U8, name="out_scales", align_bytes=64)
+        words_rows = out_1[0].rearrange("p j i -> p (j i)").bitcast(I32)
+
+        def open_banks():
+            ke = [psum.tile([P, 2, W], F32, name="ke%d" % u) for u in range(2)]
+            ve = [psum.tile([P, 2, W], F32, name="ve%d" % u) for u in range(2)]
+            return ke, ve
+
+        def products(a, h, ke, ve):
+            moving = dict(rhs=x_codes[a, h].bitcast(FP8X4), rhs_scale=x_scales[a, h])
+            for u in range(2):
+                for r in range(2):
+                    t = 2 * u + r
+                    nc.tensor.matmul_mx(
+                        out=ve[u][:, r, :],
+                        lhsT=wv4_codes[:, a, 2 * t * P : 2 * (t + 1) * P].bitcast(FP4X4),
+                        lhsT_scale=w_scales[:, a * N + t * P : a * N + (t + 1) * P],
+                        start=(a == 0 and r == 0),
+                        stop=False,
+                        **moving,
+                    )
+                    nc.tensor.matmul_mx(
+                        out=ve[u][:, r, :],
+                        lhsT=wvd_codes[a][:, t * P : (t + 1) * P].bitcast(FP8X4),
+                        lhsT_scale=wvd_scales[a][:, t * P : (t + 1) * P],
+                        start=False,
+                        stop=(a == PASSES - 1 and r == 1),
+                        **moving,
+                    )
+                for r in range(2):
+                    t = 2 * u + r
+                    nc.tensor.matmul_mx(
+                        out=ke[u][:, r, :],
+                        lhsT=wk_codes[:, a, t * P : (t + 1) * P].bitcast(FP8X4),
+                        lhsT_scale=w_scales[WK_ROW:P, a * N + t * P : a * N + (t + 1) * P],
+                        start=(a == 0 and r == 0),
+                        stop=(a == PASSES - 1 and r == 1),
+                        **moving,
+                    )
+
+        def highway(h, ke, ve):
+            cols = slice(h * W, (h + 1) * W)
+            gate = ring.tile([P, PACK, W], F32, name="gate")
+            mixed = ring.tile([P, PACK, W], F32, name="mixed", bufs=3)
+            pairs = [slice(0, 2), slice(2, 4)]
+            for u in range(2):
+                for r in range(2):
+                    t = 2 * u + r
+                    nc.scalar.activation(out=gate[:, t, :], in_=ke[u][:, r, :], func=ACT.Sigmoid, bias=bias[:, t : t + 1])
+                nc.vector.tensor_tensor(out=mixed[:, pairs[u], :], in0=ve[u][:], in1=carried[h][:, pairs[u], :], op=ALU.subtract)
+            for u in range(2):
+                nc.vector.tensor_tensor(out=mixed[:, pairs[u], :], in0=mixed[:, pairs[u], :], in1=gate[:, pairs[u], :], op=ALU.mult)
+            for u in range(2):
+                nc.vector.tensor_tensor(out=mixed[:, pairs[u], :], in0=mixed[:, pairs[u], :], in1=carried[h][:, pairs[u], :], op=ALU.add)
+            nc.sync.dma_start(out_rows[:, :, cols], mixed[:])
+            rounded = ring.tile([P, PACK * W], BF16, name="out_rounded", align_bytes=64)
+            interleave(rounded[:], mixed[:])
+            return rounded
+
+        def hand_on(h, rounded):
+            cols = slice(h * W, (h + 1) * W)
+            nc.vector.quantize_mx(out=out_codes[:, cols].bitcast(FP8X4), scales=out_scales[:, cols], in_=rounded[:])
+            nc.sync.dma_start(words_rows[:, cols], out_codes[:, cols].bitcast(I32))
+
+        gather(0, 0, 2)
+        for i in range(1, PACK):
+            gather(0, i, 1)
+        deal_packed()
+        for c0 in range(0, J, J // 2):
+            quantize_x(0, c0, J // 2)
+        gather(1, 0, 1)
+        quantize_wvd(0)
+        gather(1, 1, 1)
+        quantize_wvd(1)
+        gather(1, 2, 1)
+        banks = [open_banks(), open_banks()]
+        products(0, 0, *banks[0])
+        products(0, 1, *banks[1])
+        gather(1, 3, PARTS)
+        for h in range(PARTS):
+            quantize_x(1, h * W, W)
+        waiting = None
+        for h in range(PARTS):
+            if h >= 2:
+                banks.append(open_banks())
+                products(0, h, *banks[h])
+            products(1, h, *banks[h])
+            rounded = highway(h, *banks[h])
+            if waiting is not None:
+                hand_on(h - 1, waiting)
+            waiting = rounded
+        hand_on(PARTS - 1, waiting)
+        for q in range(4):
+            queue = nc.scalar if q % 2 else nc.sync
+            queue.dma_start(out_2[0][4 * q : 4 * q + 4, :].bitcast(I32), out_scales[32 * q : 32 * q + 4, :].bitcast(I32))

@@ -41,7 +41,7 @@ def tile_list_dl_hwayP_kernel(
         nc.gpsimd.memset(raw_scales[:].bitcast(I32), 0)
 
         head_w = held.tile([P, J], F32, name="head_w")
-        planes = [held.tile([P, T], F32, name="plane%d" % q) for q in range(PASSES * PACK)]
+        planes = [held.tile([P, T], F32, name="plane%d" % q, align_bytes=64) for q in range(PASSES * PACK)]
         x_rows = xT.rearrange("(a p i) t -> a i p t", a=PASSES, i=PACK)
 
         def load_plane(a, i):
@@ -51,7 +51,7 @@ def tile_list_dl_hwayP_kernel(
         wv4_raw = held.tile([P, PASSES, N // 2], I32, name="wv4_raw")
         wvd_raw = [held.tile([P, PACK, N], F32, name="wvd_raw%d" % a) for a in range(PASSES)]
         bias = held.tile([P, PACK], F32, name="bias")
-        carried = [held.tile([P, PACK, W], F32, name="carried%d" % h) for h in range(PARTS)]
+        carried = [held.tile([P, PACK, J // 2], F32, name="carried%d" % h) for h in range(2)]
         res_rows = res.rearrange("(p t) j -> p t j", t=PACK)
         out_rows = out_0.rearrange("(p t) j -> p t j", t=PACK)
 
@@ -70,21 +70,26 @@ def tile_list_dl_hwayP_kernel(
         nc.sync.dma_start(head_w[:, 0 : J // 2], wgt[:, 0 : J // 2])
         load_plane(0, 0)
         nc.sync.dma_start(head_w[:, J // 2 : J], wgt[:, J // 2 : J])
-        for i in range(PACK):
-            if i:
-                load_plane(0, i)
-            load_scales(wk_scales, WK_ROW, i)
-            load_scales(wv4_scales, 0, i)
+        for q in range(2):
+            load_scales(wk_scales, WK_ROW, q)
+            load_scales(wv4_scales, 0, q)
+        load_plane(0, 1)
+        for q in range(2, 4):
+            load_scales(wk_scales, WK_ROW, q)
+            load_scales(wv4_scales, 0, q)
+        load_plane(0, 2)
+        load_plane(0, 3)
         nc.sync.dma_start(bias[:], bg.rearrange("(p t) -> p t", t=PACK))
-        nc.sync.dma_start(wk_raw[:], wk_words.rearrange("a p n i -> p a (n i)").bitcast(I32))
-        nc.sync.dma_start(wv4_raw[:], wv4_words.rearrange("a p b -> p a b").bitcast(I32))
-        load_wvd(0)
         load_plane(1, 0)
+        nc.sync.dma_start(wv4_raw[:], wv4_words.rearrange("a p b -> p a b").bitcast(I32))
+        load_plane(1, 1)
+        load_wvd(0)
+        load_plane(1, 2)
         load_wvd(1)
-        for i in range(1, PACK):
-            load_plane(1, i)
-        for h in range(PARTS):
-            nc.sync.dma_start(carried[h][:], res_rows[:, :, h * W : (h + 1) * W])
+        load_plane(1, 3)
+        nc.sync.dma_start(wk_raw[:], wk_words.rearrange("a p n i -> p a (n i)").bitcast(I32))
+        for h in range(2):
+            nc.sync.dma_start(carried[h][:], res_rows[:, :, h * J // 2 : (h + 1) * J // 2])
 
         def interleave(dst, src):
             nc.scalar.copy(
@@ -106,10 +111,10 @@ def tile_list_dl_hwayP_kernel(
                     op=ALU.mult,
                 )
 
-        def quantize_x(a, c0, width):
+        def quantize_x(a, c0, width, home):
             rounded = ring.tile([P, PACK * width], BF16, name="rounded", align_bytes=64)
             interleave(rounded[:], picked[a][:, :, c0 : c0 + width])
-            codes = held.tile([P, width], U32, name="x_codes%d_%d" % (a, c0), align_bytes=64)
+            codes = held.tile([P, width], U32, name=home, align_bytes=64)
             scales = held.tile([P, width], U8, name="x_scales%d_%d" % (a, c0), align_bytes=64)
             nc.vector.quantize_mx(out=codes[:].bitcast(FP8X4), scales=scales[:], in_=rounded[:])
             for s0 in range(0, width, W):
@@ -119,15 +124,18 @@ def tile_list_dl_hwayP_kernel(
         wk_codes = held.tile([P, PASSES, N], U32, name="wk_codes", align_bytes=64)
         wv4_codes = held.tile([P, PASSES, 2 * N], U8, name="wv4_codes", align_bytes=64)
         w_scales = held.tile([P, PASSES * N], U8, name="w_scales", align_bytes=64)
-        wvd_codes = [held.tile([P, N], U32, name="wvd_codes%d" % a, align_bytes=64) for a in range(PASSES)]
+        wvd_codes = {}
         wvd_scales = [held.tile([P, N], U8, name="wvd_scales%d" % a, align_bytes=64) for a in range(PASSES)]
 
-        def deal_packed():
+        def deal_wk():
             for a in range(PASSES):
                 nc.scalar.copy(
                     out=wk_codes[:, a, :].rearrange("p (t c u) -> p c t u", t=PACK, u=4),
                     in_=wk_raw[:, a, :].bitcast(U32).rearrange("p (c u t) -> p c t u", t=PACK, u=4),
                 )
+
+        def deal_packed():
+            for a in range(PASSES):
                 nc.scalar.copy(
                     out=wv4_codes[:, a, :].bitcast(U16).rearrange("p (t c u) -> p c t u", t=PACK, u=8),
                     in_=wv4_raw[:, a, :].bitcast(U16).rearrange("p (c u t) -> p c t u", t=PACK, u=8),
@@ -143,6 +151,7 @@ def tile_list_dl_hwayP_kernel(
                 out=rounded[:].rearrange("p (t m i) -> p m i t", t=PACK, i=PACK),
                 in_=wvd_raw[a][:].rearrange("p i (m t) -> p m i t", t=PACK),
             )
+            wvd_codes[a] = held.tile([P, N], U32, name="plane%d" % (6 + a), align_bytes=64)
             nc.vector.quantize_mx(out=wvd_codes[a][:].bitcast(FP8X4), scales=wvd_scales[a][:], in_=rounded[:])
 
         out_codes = held.tile([P, J], U32, name="out_codes", align_bytes=64)
@@ -154,90 +163,102 @@ def tile_list_dl_hwayP_kernel(
             ve = [psum.tile([P, 2, W], F32, name="ve%d" % u) for u in range(2)]
             return ke, ve
 
-        def products(a, h, ke, ve):
+        def value_products(a, h, ve):
             moving = dict(rhs=x_codes[a, h].bitcast(FP8X4), rhs_scale=x_scales[a, h])
-            for u in range(2):
-                for r in range(2):
-                    t = 2 * u + r
-                    nc.tensor.matmul_mx(
-                        out=ve[u][:, r, :],
-                        lhsT=wv4_codes[:, a, 2 * t * P : 2 * (t + 1) * P].bitcast(FP4X4),
-                        lhsT_scale=w_scales[:, a * N + t * P : a * N + (t + 1) * P],
-                        start=(a == 0 and r == 0),
-                        stop=False,
-                        **moving,
-                    )
-                    nc.tensor.matmul_mx(
-                        out=ve[u][:, r, :],
-                        lhsT=wvd_codes[a][:, t * P : (t + 1) * P].bitcast(FP8X4),
-                        lhsT_scale=wvd_scales[a][:, t * P : (t + 1) * P],
-                        start=False,
-                        stop=(a == PASSES - 1 and r == 1),
-                        **moving,
-                    )
-                for r in range(2):
-                    t = 2 * u + r
+            for t in range(PACK):
+                u, r = divmod(t, 2)
+                nc.tensor.matmul_mx(
+                    out=ve[u][:, r, :],
+                    lhsT=wv4_codes[:, a, 2 * t * P : 2 * (t + 1) * P].bitcast(FP4X4),
+                    lhsT_scale=w_scales[:, a * N + t * P : a * N + (t + 1) * P],
+                    start=(a == 0 and r == 0),
+                    stop=False,
+                    **moving,
+                )
+                nc.tensor.matmul_mx(
+                    out=ve[u][:, r, :],
+                    lhsT=wvd_codes[a][:, t * P : (t + 1) * P].bitcast(FP8X4),
+                    lhsT_scale=wvd_scales[a][:, t * P : (t + 1) * P],
+                    start=False,
+                    stop=(a == PASSES - 1 and r == 1),
+                    **moving,
+                )
+
+        def gate_products(h, ke):
+            for t in range(PACK):
+                u, r = divmod(t, 2)
+                for a in range(PASSES):
                     nc.tensor.matmul_mx(
                         out=ke[u][:, r, :],
                         lhsT=wk_codes[:, a, t * P : (t + 1) * P].bitcast(FP8X4),
                         lhsT_scale=w_scales[WK_ROW:P, a * N + t * P : a * N + (t + 1) * P],
-                        start=(a == 0 and r == 0),
-                        stop=(a == PASSES - 1 and r == 1),
-                        **moving,
+                        rhs=x_codes[a, h].bitcast(FP8X4),
+                        rhs_scale=x_scales[a, h],
+                        start=(a == 0),
+                        stop=(a == PASSES - 1),
                     )
 
-        def highway(h, ke, ve):
-            cols = slice(h * W, (h + 1) * W)
+        def highway(h, ke, ve, pieces):
             gate = ring.tile([P, PACK, W], F32, name="gate")
             mixed = ring.tile([P, PACK, W], F32, name="mixed", bufs=3)
+            stream = carried[h // 2][:, :, (h % 2) * W : (h % 2 + 1) * W]
             pairs = [slice(0, 2), slice(2, 4)]
             for u in range(2):
                 for r in range(2):
                     t = 2 * u + r
                     nc.scalar.activation(out=gate[:, t, :], in_=ke[u][:, r, :], func=ACT.Sigmoid, bias=bias[:, t : t + 1])
-                nc.vector.tensor_tensor(out=mixed[:, pairs[u], :], in0=ve[u][:], in1=carried[h][:, pairs[u], :], op=ALU.subtract)
-            for u in range(2):
-                nc.vector.tensor_tensor(out=mixed[:, pairs[u], :], in0=mixed[:, pairs[u], :], in1=gate[:, pairs[u], :], op=ALU.mult)
-            for u in range(2):
-                nc.vector.tensor_tensor(out=mixed[:, pairs[u], :], in0=mixed[:, pairs[u], :], in1=carried[h][:, pairs[u], :], op=ALU.add)
-            nc.sync.dma_start(out_rows[:, :, cols], mixed[:])
-            rounded = ring.tile([P, PACK * W], BF16, name="out_rounded", align_bytes=64)
-            interleave(rounded[:], mixed[:])
-            return rounded
+                nc.vector.tensor_tensor(out=mixed[:, pairs[u], :], in0=ve[u][:], in1=stream[:, pairs[u], :], op=ALU.subtract)
+            done = []
+            width = W // pieces
+            for c0 in range(0, W, width):
+                part = slice(c0, c0 + width)
+                cols = slice(h * W + c0, h * W + c0 + width)
+                for u in range(2):
+                    nc.vector.tensor_tensor(out=mixed[:, pairs[u], part], in0=mixed[:, pairs[u], part], in1=gate[:, pairs[u], part], op=ALU.mult)
+                for u in range(2):
+                    nc.vector.tensor_tensor(out=mixed[:, pairs[u], part], in0=mixed[:, pairs[u], part], in1=stream[:, pairs[u], part], op=ALU.add)
+                nc.sync.dma_start(out_rows[:, :, cols], mixed[:, :, part])
+                rounded = ring.tile([P, PACK * width], BF16, name="out_rounded", align_bytes=64, bufs=3)
+                interleave(rounded[:], mixed[:, :, part])
+                done.append((cols, rounded))
+            return done
 
-        def hand_on(h, rounded):
-            cols = slice(h * W, (h + 1) * W)
+        def hand_on(cols, rounded):
             nc.vector.quantize_mx(out=out_codes[:, cols].bitcast(FP8X4), scales=out_scales[:, cols], in_=rounded[:])
             nc.sync.dma_start(words_rows[:, cols], out_codes[:, cols].bitcast(I32))
 
         gather(0, 0, 2)
         for i in range(1, PACK):
             gather(0, i, 1)
-        deal_packed()
-        for c0 in range(0, J, J // 2):
-            quantize_x(0, c0, J // 2)
         gather(1, 0, 1)
-        quantize_wvd(0)
+        quantize_x(0, 0, J // 2, "plane4")
         gather(1, 1, 1)
-        quantize_wvd(1)
+        quantize_x(0, J // 2, J // 2, "plane5")
+        deal_packed()
         gather(1, 2, 1)
-        banks = [open_banks(), open_banks()]
-        products(0, 0, *banks[0])
-        products(0, 1, *banks[1])
+        quantize_wvd(0)
         gather(1, 3, PARTS)
+        quantize_wvd(1)
+        banks = [open_banks(), open_banks()]
+        value_products(0, 0, banks[0][1])
+        value_products(0, 1, banks[1][1])
+        quantize_x(1, 0, W, "plane0")
+        deal_wk()
+        waiting = []
         for h in range(PARTS):
-            quantize_x(1, h * W, W)
-        waiting = None
-        for h in range(PARTS):
+            if h + 1 < PARTS:
+                quantize_x(1, (h + 1) * W, W, "plane%d" % (h + 1))
             if h >= 2:
                 banks.append(open_banks())
-                products(0, h, *banks[h])
-            products(1, h, *banks[h])
-            rounded = highway(h, *banks[h])
-            if waiting is not None:
-                hand_on(h - 1, waiting)
-            waiting = rounded
-        hand_on(PARTS - 1, waiting)
+                value_products(0, h, banks[h][1])
+            value_products(1, h, banks[h][1])
+            gate_products(h, banks[h][0])
+            done = highway(h, *banks[h], 2 if h == PARTS - 1 else 1)
+            for piece in waiting:
+                hand_on(*piece)
+            waiting = done
+        for piece in waiting:
+            hand_on(*piece)
         for q in range(4):
             queue = nc.scalar if q % 2 else nc.sync
             queue.dma_start(out_2[0][4 * q : 4 * q + 4, :].bitcast(I32), out_scales[32 * q : 32 * q + 4, :].bitcast(I32))

from contextlib import ExitStack

import concourse.mybir as mybir

K, N, T, J = 1024, 512, 2048, 1024
FLOPS = 3 * 2 * K * N * J

F32 = mybir.dt.float32
BF16 = mybir.dt.bfloat16
I32 = mybir.dt.int32
U32 = mybir.dt.uint32
U16 = mybir.dt.uint16
U8 = mybir.dt.uint8
FP8X4 = mybir.dt.float8_e4m3fn_x4
FP4X4 = mybir.dt.float4_e2m1fn_x4
ALU = mybir.AluOpType
ACT = mybir.ActivationFunctionType

P = 128
PACK = 4
K_PASS = P * PACK
PASSES = K // K_PASS
W = 256
PARTS = J // W
WK_ROW = 4


def tile_list_dl_hwayP_kernel(
    tc, xT, wgt, wk_words, wk_scales, wv4_words, wv4_scales, wvd, bg, res, offs, out_0, out_1, out_2
):
    nc = tc.nc
    with ExitStack() as ctx:
        held = ctx.enter_context(tc.tile_pool(name="held", bufs=1))
        ring = ctx.enter_context(tc.tile_pool(name="ring", bufs=2))
        psum = ctx.enter_context(tc.psum_pool(name="psum", bufs=2))

        offsets = held.tile([P, J // 16], U16, name="offsets")
        nc.sync.dma_start(offsets[:], offs)

        raw_scales = held.tile([P, PASSES * N], U8, name="raw_scales", align_bytes=64)
        nc.gpsimd.memset(raw_scales[:].bitcast(I32), 0)

        head_w = held.tile([P, J], F32, name="head_w")
        planes = [held.tile([P, T], F32, name="plane%d" % q, align_bytes=64) for q in range(PASSES * PACK)]
        x_rows = xT.rearrange("(a p i) t -> a i p t", a=PASSES, i=PACK)

        def load_plane(a, i):
            nc.sync.dma_start(planes[PACK * a + i][:], x_rows[a, i])

        wk_raw = held.tile([P, PASSES, N], I32, name="wk_raw")
        wv4_raw = held.tile([P, PASSES, N // 2], I32, name="wv4_raw")
        wvd_raw = [held.tile([P, PACK, N], F32, name="wvd_raw%d" % a) for a in range(PASSES)]
        bias = held.tile([P, PACK], F32, name="bias")
        carried = [held.tile([P, PACK, J // 2], F32, name="carried%d" % h) for h in range(2)]
        res_rows = res.rearrange("(p t) j -> p t j", t=PACK)
        out_rows = out_0.rearrange("(p t) j -> p t j", t=PACK)

        def load_scales(src, row0, q):
            dst = raw_scales[32 * q + row0 : 32 * q + row0 + 4, :].bitcast(I32)
            nc.sync.dma_start(
                dst.rearrange("r (a n) -> r a n", a=PASSES),
                src[:, 4 * q : 4 * q + 4, :].bitcast(I32).rearrange("a r n -> r a n"),
            )

        def load_wvd(a):
            nc.sync.dma_start(
                wvd_raw[a][:], wvd[a * K_PASS : (a + 1) * K_PASS, :].rearrange("(p i) n -> p i n", i=PACK)
            )

        nc.sync.dma_start(head_w[:, 0 : J // 2], wgt[:, 0 : J // 2])
        load_plane(0, 0)
        nc.sync.dma_start(head_w[:, J // 2 : J], wgt[:, J // 2 : J])
        for q in range(2):
            load_scales(wk_scales, WK_ROW, q)
            load_scales(wv4_scales, 0, q)
        load_plane(0, 1)
        for q in range(2, 4):
            load_scales(wk_scales, WK_ROW, q)
            load_scales(wv4_scales, 0, q)
        load_plane(0, 2)
        load_plane(0, 3)
        nc.sync.dma_start(bias[:], bg.rearrange("(p t) -> p t", t=PACK))
        load_plane(1, 0)
        nc.sync.dma_start(wv4_raw[:], wv4_words.rearrange("a p b -> p a b").bitcast(I32))
        load_plane(1, 1)
        load_wvd(0)
        load_plane(1, 2)
        load_wvd(1)
        load_plane(1, 3)
        nc.sync.dma_start(wk_raw[:], wk_words.rearrange("a p n i -> p a (n i)").bitcast(I32))
        for h in range(2):
            nc.sync.dma_start(carried[h][:], res_rows[:, :, h * J // 2 : (h + 1) * J // 2])

        def interleave(dst, src):
            nc.scalar.copy(
                out=dst.rearrange("p (c u i) -> p c i u", u=4, i=PACK),
                in_=src.rearrange("p i (c u) -> p c i u", u=4),
            )

        picked = [held.tile([P, PACK, J], F32, name="picked%d" % a) for a in range(PASSES)]
        x_codes = {}
        x_scales = {}

        def gather(a, i, pieces):
            width = J // pieces
            for c0 in range(0, J, width):
                nc.vector.tensor_tensor(
                    out=picked[a][:, i, c0 : c0 + width],
                    in0=planes[PACK * a + i][:].indirect(offsets[:, c0 // 16 : (c0 + width) // 16]),
                    in1=head_w[:, c0 : c0 + width],
                    op=ALU.mult,
                )

        def quantize_x(a, c0, width, home):
            rounded = ring.tile([P, PACK * width], BF16, name="rounded", align_bytes=64)
            interleave(rounded[:], picked[a][:, :, c0 : c0 + width])
            codes = held.tile([P, width], U32, name=home, align_bytes=64)
            scales = held.tile([P, width], U8, name="x_scales%d_%d" % (a, c0), align_bytes=64)
            nc.vector.quantize_mx(out=codes[:].bitcast(FP8X4), scales=scales[:], in_=rounded[:])
            for s0 in range(0, width, W):
                x_codes[a, (c0 + s0) // W] = codes[:, s0 : s0 + W]
                x_scales[a, (c0 + s0) // W] = scales[:, s0 : s0 + W]

        wk_codes = held.tile([P, PASSES, N], U32, name="wk_codes", align_bytes=64)
        wv4_codes = held.tile([P, PASSES, 2 * N], U8, name="wv4_codes", align_bytes=64)
        w_scales = held.tile([P, PASSES * N], U8, name="w_scales", align_bytes=64)
        wvd_codes = {}
        wvd_scales = [held.tile([P, N], U8, name="wvd_scales%d" % a, align_bytes=64) for a in range(PASSES)]

        def deal_wk():
            for a in range(PASSES):
                nc.scalar.copy(
                    out=wk_codes[:, a, :].rearrange("p (t c u) -> p c t u", t=PACK, u=4),
                    in_=wk_raw[:, a, :].bitcast(U32).rearrange("p (c u t) -> p c t u", t=PACK, u=4),
                )

        def deal_packed():
            for a in range(PASSES):
                nc.scalar.copy(
                    out=wv4_codes[:, a, :].bitcast(U16).rearrange("p (t c u) -> p c t u", t=PACK, u=8),
                    in_=wv4_raw[:, a, :].bitcast(U16).rearrange("p (c u t) -> p c t u", t=PACK, u=8),
                )
            nc.vector.tensor_copy(
                out=w_scales[:].rearrange("p (a t c u) -> p a c t u", a=PASSES, t=PACK, u=16),
                in_=raw_scales[:].rearrange("p (a c u t) -> p a c t u", a=PASSES, t=PACK, u=16),
            )

        def quantize_wvd(a):
            rounded = ring.tile([P, PACK * N], BF16, name="rounded", align_bytes=64)
            nc.scalar.copy(
                out=rounded[:].rearrange("p (t m i) -> p m i t", t=PACK, i=PACK),
                in_=wvd_raw[a][:].rearrange("p i (m t) -> p m i t", t=PACK),
            )
            wvd_codes[a] = held.tile([P, N], U32, name="plane%d" % (6 + a), align_bytes=64)
            nc.vector.quantize_mx(out=wvd_codes[a][:].bitcast(FP8X4), scales=wvd_scales[a][:], in_=rounded[:])

        out_codes = held.tile([P, J], U32, name="out_codes", align_bytes=64)
        out_scales = held.tile([P, J], U8, name="out_scales", align_bytes=64)
        words_rows = out_1[0].rearrange("p j i -> p (j i)").bitcast(I32)

        def open_banks():
            ke = [psum.tile([P, 2, W], F32, name="ke%d" % u) for u in range(2)]
            ve = [psum.tile([P, 2, W], F32, name="ve%d" % u) for u in range(2)]
            return ke, ve

        def value_products(a, h, ve):
            moving = dict(rhs=x_codes[a, h].bitcast(FP8X4), rhs_scale=x_scales[a, h])
            for t in range(PACK):
                u, r = divmod(t, 2)
                nc.tensor.matmul_mx(
                    out=ve[u][:, r, :],
                    lhsT=wv4_codes[:, a, 2 * t * P : 2 * (t + 1) * P].bitcast(FP4X4),
                    lhsT_scale=w_scales[:, a * N + t * P : a * N + (t + 1) * P],
                    start=(a == 0 and r == 0),
                    stop=False,
                    **moving,
                )
                nc.tensor.matmul_mx(
                    out=ve[u][:, r, :],
                    lhsT=wvd_codes[a][:, t * P : (t + 1) * P].bitcast(FP8X4),
                    lhsT_scale=wvd_scales[a][:, t * P : (t + 1) * P],
                    start=False,
                    stop=(a == PASSES - 1 and r == 1),
                    **moving,
                )

        def gate_products(h, ke):
            for t in range(PACK):
                u, r = divmod(t, 2)
                for a in range(PASSES):
                    nc.tensor.matmul_mx(
                        out=ke[u][:, r, :],
                        lhsT=wk_codes[:, a, t * P : (t + 1) * P].bitcast(FP8X4),
                        lhsT_scale=w_scales[WK_ROW:P, a * N + t * P : a * N + (t + 1) * P],
                        rhs=x_codes[a, h].bitcast(FP8X4),
                        rhs_scale=x_scales[a, h],
                        start=(a == 0),
                        stop=(a == PASSES - 1),
                    )

        def highway(h, ke, ve, pieces):
            gate = ring.tile([P, PACK, W], F32, name="gate")
            mixed = ring.tile([P, PACK, W], F32, name="mixed", bufs=3)
            stream = carried[h // 2][:, :, (h % 2) * W : (h % 2 + 1) * W]
            pairs = [slice(0, 2), slice(2, 4)]
            for u in range(2):
                for r in range(2):
                    t = 2 * u + r
                    nc.scalar.activation(out=gate[:, t, :], in_=ke[u][:, r, :], func=ACT.Sigmoid, bias=bias[:, t : t + 1])
                nc.vector.tensor_tensor(out=mixed[:, pairs[u], :], in0=ve[u][:], in1=stream[:, pairs[u], :], op=ALU.subtract)
            done = []
            width = W // pieces
            for c0 in range(0, W, width):
                part = slice(c0, c0 + width)
                cols = slice(h * W + c0, h * W + c0 + width)
                for u in range(2):
                    nc.vector.tensor_tensor(out=mixed[:, pairs[u], part], in0=mixed[:, pairs[u], part], in1=gate[:, pairs[u], part], op=ALU.mult)
                for u in range(2):
                    nc.vector.tensor_tensor(out=mixed[:, pairs[u], part], in0=mixed[:, pairs[u], part], in1=stream[:, pairs[u], part], op=ALU.add)
                nc.sync.dma_start(out_rows[:, :, cols], mixed[:, :, part])
                rounded = ring.tile([P, PACK * width], BF16, name="out_rounded", align_bytes=64, bufs=3)
                interleave(rounded[:], mixed[:, :, part])
                done.append((cols, rounded))
            return done

        def hand_on(cols, rounded):
            nc.vector.quantize_mx(out=out_codes[:, cols].bitcast(FP8X4), scales=out_scales[:, cols], in_=rounded[:])
            nc.sync.dma_start(words_rows[:, cols], out_codes[:, cols].bitcast(I32))

        gather(0, 0, 2)
        for i in range(1, PACK):
            gather(0, i, 1)
        gather(1, 0, 1)
        quantize_x(0, 0, J // 2, "plane4")
        gather(1, 1, 1)
        quantize_x(0, J // 2, J // 2, "plane5")
        deal_packed()
        gather(1, 2, 1)
        quantize_wvd(0)
        gather(1, 3, PARTS)
        quantize_wvd(1)
        banks = [open_banks(), open_banks()]
        value_products(0, 0, banks[0][1])
        value_products(0, 1, banks[1][1])
        quantize_x(1, 0, W, "plane0")
        deal_wk()
        waiting = []
        for h in range(PARTS):
            if h + 1 < PARTS:
                quantize_x(1, (h + 1) * W, W, "plane%d" % (h + 1))
            if h >= 2:
                banks.append(open_banks())
                value_products(0, h, banks[h][1])
            value_products(1, h, banks[h][1])
            gate_products(h, banks[h][0])
            done = highway(h, *banks[h], 2 if h == PARTS - 1 else 1)
            for piece in waiting:
                hand_on(*piece)
            waiting = done
        for piece in waiting:
            hand_on(*piece)
        for q in range(4):
            queue = nc.scalar if q % 2 else nc.sync
            queue.dma_start(out_2[0][4 * q : 4 * q + 4, :].bitcast(I32), out_scales[32 * q : 32 * q + 4, :].bitcast(I32))
